import numpy as np
import ml_dtypes


def mxq(x, axis, fmt="e4m3"):
    dtype, down = {"e4m3": (ml_dtypes.float8_e4m3fn, 7), "e5m2": (ml_dtypes.float8_e5m2, 14)}[fmt]
    v = np.moveaxis(np.asarray(x, np.float32).astype(ml_dtypes.bfloat16).astype(np.float64), axis, -1)
    blocks = v.reshape(v.shape[:-1] + (-1, 32))
    amax = np.abs(blocks).max(-1, keepdims=True)
    byte = np.maximum(np.where(amax > 0, np.frexp(amax)[1] - 1 + 127, 0) - down, 1)
    scale = np.exp2(byte - 127.0)
    codes = (blocks / scale).astype(np.float32).astype(dtype).astype(np.float64)
    return np.moveaxis((codes * scale).reshape(v.shape), -1, axis)


WIDE = False


def mx_kscale(k):
    if not WIDE:
        return np.ones(k)
    levels = np.array([10, -10, 5, -5, 0])
    if k % 512:
        return np.exp2(np.random.permutation(np.resize(levels, k // 32))).repeat(32)
    a = np.empty((k // 512, 16))
    for p in range(k // 512):
        a[p, :8] = np.random.permutation(np.resize(levels, 8))
        for g in range(8):
            far = levels[np.abs(levels - a[p, g]) >= 10]
            a[p, g + 8] = far[np.random.randint(len(far))]
    return np.exp2(a.ravel()).repeat(32)


def f64(x):
    return np.asarray(x).astype(np.float64)


def striped(idx):
    return np.tile(np.asarray(idx).reshape(-1, 16).T, (8, 1)).astype(np.uint16)


def unstriped(offs):
    return offs[:16].T.reshape(-1).astype(np.int64)


E2M1 = np.array([0.0, 0.5, 1.0, 1.5, 2.0, 3.0, 4.0, 6.0, -0.0, -0.5, -1.0, -1.5, -2.0, -3.0, -4.0, -6.0])


def pack_weight(w, fmt):
    k, n = w.shape
    w = f64(np.asarray(w, np.float32).astype(ml_dtypes.bfloat16)).reshape(k // 32, 32, n)
    amax = np.abs(w).max(1)
    if fmt == "e4m3":
        byte = np.frexp(amax)[1] - 1 + 127 - 7
    else:
        mant, ex = np.frexp(amax / 6.0)
        byte = np.where(mant > 0.5, ex, ex - 1) + 127
    byte = np.clip(np.where(amax > 0, byte, 1), 1, 254)
    scaled = (w * np.exp2(127.0 - byte)[:, None, :]).reshape(k, n).astype(np.float32)
    by_word = np.ascontiguousarray(scaled.reshape(k // 512, 128, 4, n).transpose(0, 1, 3, 2))
    if fmt == "e4m3":
        words = by_word.astype(ml_dtypes.float8_e4m3fn).view(np.uint8)
    else:
        c = by_word.astype(ml_dtypes.float4_e2m1fn).view(np.uint8) & 0xF
        words = (c[..., 0::2] | (c[..., 1::2] << 4)).reshape(k // 512, 128, 2 * n)
    return np.ascontiguousarray(words), np.ascontiguousarray(byte.astype(np.uint8).reshape(k // 512, 16, n))


def unpack_weight(words, scales, fmt):
    g, _, n = scales.shape
    words = np.ascontiguousarray(words).reshape(g, 128, n, -1)
    if fmt == "e4m3":
        vals = words.view(ml_dtypes.float8_e4m3fn).astype(np.float64)
    else:
        nib = np.empty((g, 128, n, 4), np.uint8)
        nib[..., 0::2] = words & 0xF
        nib[..., 1::2] = words >> 4
        vals = E2M1[nib]
    vals = vals * np.repeat(np.exp2(scales.astype(np.float64) - 127.0), 8, axis=1)[..., None]
    return vals.transpose(0, 1, 3, 2).reshape(g * 512, n)


D, E, T, I, Q, G, U = 512, 512, 1024, 256, 512, 32, 1024


def setup_inputs():
    n = np.random.standard_normal
    idx = np.random.permutation(T)[:I]
    idx4 = np.random.permutation(U)[:I]
    fd = mx_kscale(D)
    fe = mx_kscale(E)
    fq = mx_kscale(Q)
    keysp = pack_weight(n((D, T)) / fd[:, None], "e2m1")
    valsp = pack_weight(n((E, T)) / fe[:, None], "e2m1")
    return {
        "query": (n((D, Q)) * 0.6 / np.sqrt(D) * fd[:, None]).astype(np.float32),
        "keys_words": keysp[0],
        "keys_scales": keysp[1],
        "pw": (np.random.uniform(0.5, 1.6, (Q, 1))).astype(np.float32),
        "gout": (n((E, Q)) * 1 / np.sqrt(E) * fe[:, None]).astype(np.float32),
        "vals_words": valsp[0],
        "vals_scales": valsp[1],
        "qs": (np.random.uniform(25.0, 100.0, (Q, 1)) * fq[:, None]).astype(np.float32),
        "qrows": (n((Q, D)) / fq[:, None]).astype(np.float32),
        "old": (n((D, U)) * 4.0).astype(np.float32),
        "fade": (np.random.uniform(0.5, 1.0, (1, U))).astype(np.float32),
        "offs": striped(idx),
        "offs4": striped(idx4),
    }


def reference(query, keys_words, keys_scales, pw, gout, vals_words, vals_scales, qs, qrows, old, fade, offs, offs4):
    idx = unstriped(offs)
    idx4 = unstriped(offs4)
    keysu = unpack_weight(keys_words, keys_scales, "e2m1")
    valsu = unpack_weight(vals_words, vals_scales, "e2m1")
    queryq = mxq(f64(query), 0, "e4m3")
    keysidxg = keysu[:, idx]
    a = queryq.T @ keysidxg
    x1 = np.exp(a)
    s = x1.reshape(Q, G, I // G).sum(axis=2)
    z = np.sum(x1, axis=1, keepdims=True)
    ls = np.log(s)
    lr = np.repeat(ls, I // G, axis=1)
    sr = np.repeat(s, I // G, axis=1)
    goutq = mxq(f64(gout), 0, "e4m3")
    valsidxg = valsu[:, idx]
    c0 = goutq.T @ valsidxg
    dsr = c0 / z * np.exp((a - lr) * f64(pw))
    dlr = c0 / z * sr * np.exp((a - lr) * f64(pw)) * f64(pw) * (-1.0)
    dls = dlr.reshape(Q, G, I // G).sum(axis=2)
    dz = np.sum(c0 * np.exp((a - lr) * f64(pw)) * sr / np.square(z) * (-1.0), axis=1, keepdims=True)
    ds = dsr.reshape(Q, G, I // G).sum(axis=2) + dls / s
    r1 = np.repeat(ds, I // G, axis=1)
    dx1 = dz + r1
    da = c0 / z * sr * np.exp((a - lr) * f64(pw)) * f64(pw) + dx1 * x1
    gs = da * f64(qs)
    qrowsq = mxq(f64(qrows), 0, "e4m3")
    gsq = mxq(gs, 0, "e4m3")
    gk = qrowsq.T @ gsq
    gf = np.zeros((D, U))
    gf[:, idx4] = gk
    y = f64(old) * f64(fade) + gf
    return y

@@ -1,0 +1,340 @@
+from contextlib import ExitStack
+
+import concourse.mybir as mybir
+from concourse.masks import make_identity
+
+D, E, T, I, Q, G, U = 512, 512, 1024, 256, 512, 32, 1024
+FLOPS = 2 * Q * I * D + 2 * Q * I * E + 2 * D * I * Q
+
+F32 = mybir.dt.float32
+BF16 = mybir.dt.bfloat16
+I32 = mybir.dt.int32
+U32 = mybir.dt.uint32
+U16 = mybir.dt.uint16
+U8 = mybir.dt.uint8
+FP8X4 = mybir.dt.float8_e4m3fn_x4
+FP4X4 = mybir.dt.float4_e2m1fn_x4
+ALU = mybir.AluOpType
+ACT = mybir.ActivationFunctionType
+AX = mybir.AxisListType
+
+P = 128
+PACK = 4
+PAGE = I // G
+HALF = Q // 2
+BANK = 512
+LN_FLOOR = 2.0**-60
+PW_ZERO = 2.0**-60
+
+
+def tile_attend_bsharedpower_k_kernel(
+    tc, query, keys_words, keys_scales, pw, gout, vals_words, vals_scales, qs, qrows, old, fade, offs, offs4, out
+):
+    nc = tc.nc
+    with ExitStack() as ctx:
+        sb = ctx.enter_context(tc.tile_pool(name="sb", bufs=1))
+        ps = ctx.enter_context(tc.psum_pool(name="ps", bufs=1))
+
+        def bank(k, name):
+            return ps.tile([P, BANK], F32, name=name, tag=f"bank{k}")
+
+        def pages(ap):
+            return ap.rearrange("p (g j) -> p g j", j=PAGE)
+
+        def over_slots(ap):
+            return ap.unsqueeze(2).to_broadcast([P, G, PAGE])
+
+        def over_pages(ap):
+            return ap.unsqueeze(2).to_broadcast([P, ap.shape[1], G])
+
+        k_plane = sb.tile([P, T], U8, name="k_plane", align_bytes=64)
+        v_plane = sb.tile([P, T], U8, name="v_plane", align_bytes=64)
+        nc.gpsimd.memset(k_plane[:].bitcast(I32), 0)
+        nc.gpsimd.memset(v_plane[:].bitcast(I32), 0)
+        fade_rows = sb.tile([P, P], F32, name="fade_rows")
+        nc.vector.memset(fade_rows[:], 0.0)
+        ln_floor = sb.tile([P, 1], F32, name="ln_floor")
+        nc.vector.memset(ln_floor[:], LN_FLOOR)
+
+        slots = sb.tile([P, I // 16], U16, name="slots")
+        nc.sync.dma_start(slots[:], offs)
+        k_words = sb.tile([P, T], U16, name="k_words", align_bytes=64)
+        v_words = sb.tile([P, T], U16, name="v_words", align_bytes=64)
+        nc.sync.dma_start(k_words[:].bitcast(I32), keys_words[0].bitcast(I32))
+        nc.sync.dma_start(v_words[:].bitcast(I32), vals_words[0].bitcast(I32))
+        for quad in range(4):
+            nc.sync.dma_start(
+                k_plane[32 * quad : 32 * quad + 4, :].bitcast(I32),
+                keys_scales[0, 4 * quad : 4 * quad + 4, :].bitcast(I32),
+            )
+
+        def load_halves(src, name):
+            rows = src.rearrange("(p j) q -> p j q", j=PACK)
+            halves = [sb.tile([P, PACK, HALF], F32, name=f"{name}{h}") for h in range(2)]
+            for h in range(2):
+                nc.sync.dma_start(halves[h][:], rows[:, :, h * HALF : (h + 1) * HALF])
+            return halves
+
+        query_raw = load_halves(query, "query_raw")
+        for quad in range(4):
+            nc.sync.dma_start(
+                v_plane[32 * quad : 32 * quad + 4, :].bitcast(I32),
+                vals_scales[0, 4 * quad : 4 * quad + 4, :].bitcast(I32),
+            )
+        gout_raw = load_halves(gout, "gout_raw")
+        pw_raw = sb.tile([P, PACK], F32, name="pw_raw")
+        nc.sync.dma_start(pw_raw[:], pw.rearrange("(p r) o -> p (r o)", r=PACK))
+        qs_sb = sb.tile([P, PACK], F32, name="qs_sb")
+        nc.sync.dma_start(qs_sb[:], qs.rearrange("(p r) o -> p (r o)", r=PACK))
+        qrows_raw = sb.tile([P, PACK, D], F32, name="qrows_raw")
+        nc.sync.dma_start(qrows_raw[:], qrows.rearrange("(p j) d -> p j d", j=PACK))
+        places = sb.tile([P, I // 16], U16, name="places")
+        nc.sync.dma_start(places[:], offs4)
+        nc.sync.dma_start(fade_rows[0 : U // P, :], fade.rearrange("o (c u) -> (o c) u", u=P))
+        old_rows = old.rearrange("(t p) u -> p t u", p=P)
+        old_sb = [sb.tile([P, 4, BANK], F32, name=f"old_sb{h}") for h in range(2)]
+        for h in range(2):
+            nc.sync.dma_start(old_sb[h][:], old_rows[:, :, h * BANK : (h + 1) * BANK])
+
+        ident = sb.tile([P, P], F32, name="ident")
+        make_identity(nc, ident[:])
+        windows = [sb.tile([P, U], F32, name=f"window{w}") for w in range(2)]
+        for w in range(2):
+            nc.gpsimd.memset(windows[w][:], 0.0)
+
+        kg_words = sb.tile([P, I], U16, name="kg_words", align_bytes=64)
+        vg_words = sb.tile([P, I], U16, name="vg_words", align_bytes=64)
+        kg_plane = sb.tile([P, I], U8, name="kg_plane", align_bytes=64)
+        vg_plane = sb.tile([P, I], U8, name="vg_plane", align_bytes=64)
+        nc.vector.tensor_copy(kg_words[:], k_words[:].indirect(slots[:]))
+        nc.vector.tensor_copy(vg_words[:], v_words[:].indirect(slots[:]))
+        nc.vector.tensor_copy(kg_plane[:], k_plane[:].indirect(slots[:]))
+        nc.vector.tensor_copy(vg_plane[:], v_plane[:].indirect(slots[:]))
+
+        def deal(copy, raw, grouped, h):
+            s0 = h * HALF // PACK
+            copy(
+                grouped[:, :, s0 : s0 + HALF // PACK, :].rearrange("p r s j -> p s j r"),
+                raw[:].rearrange("p j (s r) -> p s j r", r=PACK),
+            )
+
+        def quantise(grouped, name):
+            codes = sb.tile([P, PACK, P], U32, name=f"{name}_codes", align_bytes=64)
+            plane = sb.tile([P, PACK, P], U8, name=f"{name}_plane", align_bytes=64)
+            for r in range(PACK):
+                nc.vector.quantize_mx(
+                    out=codes[:, r, :].bitcast(FP8X4),
+                    scales=plane[:, r, :],
+                    in_=grouped[:, r, :, :].rearrange("p s j -> p (s j)"),
+                )
+            return codes, plane
+
+        query_bf = sb.tile([P, PACK, P, PACK], BF16, name="query_bf", align_bytes=64)
+        deal(nc.scalar.copy, query_raw[0], query_bf, 0)
+        deal(nc.vector.tensor_copy, query_raw[1], query_bf, 1)
+        q_codes, q_plane = quantise(query_bf, "query")
+        a_ps = [bank(r, f"a_ps{r}") for r in range(PACK)]
+        for r in range(PACK):
+            nc.tensor.matmul_mx(
+                out=a_ps[r][:, 0:I],
+                lhsT=q_codes[:, r, :].bitcast(FP8X4),
+                lhsT_scale=q_plane[:, r, :],
+                rhs=kg_words[:].bitcast(FP4X4),
+                rhs_scale=kg_plane[:],
+                start=True,
+                stop=True,
+            )
+
+        neg_max = sb.tile([P, PACK], F32, name="neg_max")
+        z = sb.tile([P, PACK], F32, name="z")
+        x1 = sb.tile([P, PACK, I], F32, name="x1")
+        for r in range(PACK):
+            nc.vector.tensor_reduce(neg_max[:, r : r + 1], a_ps[r][:, 0:I], AX.X, ALU.max, negate=True)
+            nc.scalar.activation(
+                x1[:, r, :], a_ps[r][:, 0:I], ACT.Exp, bias=neg_max[:, r : r + 1], accum_out=z[:, r : r + 1]
+            )
+        s = sb.tile([P, PACK, G], F32, name="s")
+        for h in range(2):
+            nc.vector.tensor_reduce(
+                s[:, 2 * h : 2 * h + 2, :].rearrange("p r g -> p (r g)"),
+                x1[:, 2 * h : 2 * h + 2, :].rearrange("p r (g j) -> p (r g) j", j=PAGE),
+                AX.X,
+                ALU.add,
+            )
+        ls = sb.tile([P, PACK, G], F32, name="ls")
+        nc.scalar.activation(ls[:], s[:], ACT.Ln, bias=ln_floor[:])
+
+        pw_zero = sb.tile([P, PACK], F32, name="pw_zero")
+        nc.vector.tensor_scalar(pw_zero[:], pw_raw[:], 0.0, PW_ZERO, ALU.is_equal, ALU.mult)
+        power = sb.tile([P, PACK], F32, name="power")
+        nc.vector.tensor_tensor(power[:], pw_raw[:], pw_zero[:], ALU.add)
+        one_less = sb.tile([P, PACK], F32, name="one_less")
+        nc.vector.tensor_scalar(one_less[:], power[:], -1.0, 1.0, ALU.mult, ALU.add)
+        inv_power = sb.tile([P, PACK], F32, name="inv_power")
+        nc.vector.reciprocal(inv_power[:], power[:])
+        page_gain = sb.tile([P, PACK], F32, name="page_gain")
+        nc.vector.tensor_tensor(page_gain[:], one_less[:], inv_power[:], ALU.mult)
+        over_z = sb.tile([P, 2, PACK], F32, name="over_z")
+        nc.vector.tensor_tensor(over_z[:, 0, :], qs_sb[:], power[:], ALU.mult)
+        nc.vector.tensor_scalar(over_z[:, 1, :], inv_power[:], -1.0, None, ALU.mult)
+
+        gout_bf = sb.tile([P, PACK, P, PACK], BF16, name="gout_bf", align_bytes=64)
+        for h in range(2):
+            deal(nc.vector.tensor_copy, gout_raw[h], gout_bf, h)
+
+        shift = sb.tile([P, PACK], F32, name="shift")
+        nc.vector.tensor_tensor(shift[:], neg_max[:], power[:], ALU.mult)
+        inv_z = sb.tile([P, PACK], F32, name="inv_z")
+        nc.vector.reciprocal(inv_z[:], z[:])
+        gains = sb.tile([P, 2, PACK], F32, name="gains")
+        nc.vector.tensor_tensor(gains[:], over_z[:], inv_z[:].unsqueeze(1).to_broadcast([P, 2, PACK]), ALU.mult)
+
+        page_term = sb.tile([P, PACK, G], F32, name="page_term")
+        nc.vector.tensor_tensor(page_term[:], ls[:], over_pages(one_less[:]), ALU.mult)
+        expo = sb.tile([P, PACK, I], F32, name="expo", tag="expo", align_bytes=64)
+        for r in range(PACK):
+            nc.vector.scalar_tensor_tensor(
+                pages(expo[:, r, :]),
+                pages(a_ps[r][:, 0:I]),
+                power[:, r : r + 1],
+                over_slots(page_term[:, r, :]),
+                ALU.mult,
+                ALU.add,
+            )
+        g_codes, g_plane = quantise(gout_bf, "gout")
+        c_ps = [bank(4 + h, f"c_ps{h}") for h in range(2)]
+        for r in range(PACK):
+            nc.tensor.matmul_mx(
+                out=c_ps[r // 2][:, (r % 2) * I : (r % 2 + 1) * I],
+                lhsT=g_codes[:, r, :].bitcast(FP8X4),
+                lhsT_scale=g_plane[:, r, :],
+                rhs=vg_words[:].bitcast(FP4X4),
+                rhs_scale=vg_plane[:],
+                start=True,
+                stop=True,
+            )
+
+        weight = sb.tile([P, PACK, I], F32, name="weight")
+        for r in range(PACK):
+            nc.scalar.activation(weight[:, r, :], expo[:, r, :], ACT.Exp, bias=shift[:, r : r + 1])
+        inv_s = sb.tile([P, PACK, G], F32, name="inv_s")
+        nc.scalar.activation(inv_s[:], ls[:], ACT.Exp, scale=-1.0)
+
+        direct = sb.tile([P, PACK, I], F32, name="direct")
+        total = sb.tile([P, PACK], F32, name="total")
+        for r in range(PACK):
+            nc.vector.scalar_tensor_tensor(
+                direct[:, r, :],
+                c_ps[r // 2][:, (r % 2) * I : (r % 2 + 1) * I],
+                gains[:, 0, r : r + 1],
+                weight[:, r, :],
+                ALU.mult,
+                ALU.mult,
+                accum_out=total[:, r : r + 1],
+            )
+        page_factor = sb.tile([P, PACK, G], F32, name="page_factor")
+        nc.vector.tensor_tensor(page_factor[:], inv_s[:], over_pages(page_gain[:]), ALU.mult)
+        row_term = sb.tile([P, PACK], F32, name="row_term")
+        nc.vector.tensor_tensor(row_term[:], total[:], gains[:, 1, :], ALU.mult)
+        page_sum = sb.tile([P, PACK, G], F32, name="page_sum")
+        page_grad = sb.tile([P, PACK, G], F32, name="page_grad")
+        for h in range(2):
+            nc.vector.tensor_reduce(
+                page_sum[:, 2 * h : 2 * h + 2, :].rearrange("p r g -> p (r g)"),
+                direct[:, 2 * h : 2 * h + 2, :].rearrange("p r (g j) -> p (r g) j", j=PAGE),
+                AX.X,
+                ALU.add,
+            )
+        for h in range(2):
+            nc.vector.tensor_tensor(
+                page_grad[:, 2 * h : 2 * h + 2, :],
+                page_sum[:, 2 * h : 2 * h + 2, :],
+                page_factor[:, 2 * h : 2 * h + 2, :],
+                ALU.mult,
+            )
+
+        qrows_bf = sb.tile([P, D, PACK], BF16, name="qrows_bf", tag="expo", align_bytes=64)
+        nc.scalar.copy(
+            qrows_bf[:].rearrange("p (c i) j -> p c j i", i=4),
+            qrows_raw[:].rearrange("p j (c i) -> p c j i", i=4),
+        )
+        r_codes = sb.tile([P, D], U32, name="r_codes", align_bytes=64)
+        r_plane = sb.tile([P, D], U8, name="r_plane", align_bytes=64)
+
+        through = sb.tile([P, PACK, I], F32, name="through")
+        for r in range(PACK):
+            nc.vector.scalar_tensor_tensor(
+                pages(through[:, r, :]),
+                over_slots(page_grad[:, r, :]),
+                row_term[:, r : r + 1],
+                pages(x1[:, r, :]),
+                ALU.add,
+                ALU.mult,
+            )
+        gs = sb.tile([P, I, PACK], BF16, name="gs", align_bytes=64)
+        nc.vector.tensor_tensor(
+            gs[:].rearrange("p (c i) r -> p c r i", i=4),
+            direct[:].rearrange("p r (c i) -> p c r i", i=4),
+            through[:].rearrange("p r (c i) -> p c r i", i=4),
+            ALU.add,
+        )
+        nc.vector.quantize_mx(
+            out=r_codes[:].bitcast(FP8X4), scales=r_plane[:], in_=qrows_bf[:].rearrange("p d j -> p (d j)")
+        )
+        gs_codes = sb.tile([P, I], U32, name="gs_codes", align_bytes=64)
+        gs_plane = sb.tile([P, I], U8, name="gs_plane", align_bytes=64)
+        nc.vector.quantize_mx(
+            out=gs_codes[:].bitcast(FP8X4), scales=gs_plane[:], in_=gs[:].rearrange("p i r -> p (i r)")
+        )
+
+        gk = [sb.tile([P, I], F32, name=f"gk{t}") for t in range(4)]
+        for t in range(4):
+            gk_ps = bank(t % 2, f"gk_ps{t}")
+            nc.tensor.matmul_mx(
+                out=gk_ps[:, 0:I],
+                lhsT=r_codes[:, t * P : (t + 1) * P].bitcast(FP8X4),
+                lhsT_scale=r_plane[:, t * P : (t + 1) * P],
+                rhs=gs_codes[:].bitcast(FP8X4),
+                rhs_scale=gs_plane[:],
+                start=True,
+                stop=True,
+            )
+            nc.scalar.copy(gk[t][:], gk_ps[:, 0:I])
+
+        fade_ps = bank(3, "fade_ps")
+        nc.tensor.transpose(fade_ps[:, 0:P], fade_rows[:], ident[:])
+        fade_cols = sb.tile([P, U // P], F32, name="fade_cols")
+        nc.scalar.copy(fade_cols[:], fade_ps[:, 0 : U // P])
+        faded_t = [sb.tile([P, D], F32, name=f"faded_t{c}") for c in range(U // P)]
+        for c in range(U // P):
+            turned = bank(7 - c % 2, f"turned{c}")
+            for t in range(4):
+                nc.tensor.transpose(
+                    turned[:, t * P : (t + 1) * P], old_sb[c // 4][:, t, (c % 4) * P : (c % 4 + 1) * P], ident[:]
+                )
+            nc.scalar.activation(faded_t[c][:], turned[:], ACT.Copy, scale=fade_cols[:, c : c + 1])
+
+        def scatter(t):
+            nc.vector.tensor_copy(windows[t % 2][:].indirect(places[:]), gk[t][:])
+
+        def turn_back(t, h):
+            faded = bank(2 + (2 * t + h) % 6, f"faded{t}_{h}")
+            for c in range(4):
+                nc.tensor.transpose(
+                    faded[:, c * P : (c + 1) * P], faded_t[4 * h + c][:, t * P : (t + 1) * P], ident[:]
+                )
+            return faded
+
+        def finish(t):
+            result = sb.tile([P, U], F32, name=f"result{t}")
+            for h in range(2):
+                cols = slice(h * BANK, (h + 1) * BANK)
+                faded = turn_back(t, h)
+                nc.vector.tensor_tensor(result[:, cols], faded[:], windows[t % 2][:, cols], ALU.add)
+                nc.sync.dma_start(out[t * P : (t + 1) * P, cols], result[:, cols])
+
+        scatter(0)
+        for t in range(1, 4):
+            scatter(t)
+            finish(t - 1)
+        finish(3)

@@ -25,6 +25,9 @@ HALF = Q // 2
 BANK = 512
 LN_FLOOR = 2.0**-60
 PW_ZERO = 2.0**-60
+ON_GPSIMD = 4
+TURN_BANKS = (6, 7, 0, 1)
+BACK_BANKS = (2, 6, 7, 0, 1, 6, 7, 0)
 
 
 def tile_attend_bsharedpower_k_kernel(
@@ -61,7 +64,6 @@ def tile_attend_bsharedpower_k_kernel(
         k_words = sb.tile([P, T], U16, name="k_words", align_bytes=64)
         v_words = sb.tile([P, T], U16, name="v_words", align_bytes=64)
         nc.sync.dma_start(k_words[:].bitcast(I32), keys_words[0].bitcast(I32))
-        nc.sync.dma_start(v_words[:].bitcast(I32), vals_words[0].bitcast(I32))
         for quad in range(4):
             nc.sync.dma_start(
                 k_plane[32 * quad : 32 * quad + 4, :].bitcast(I32),
@@ -76,16 +78,17 @@ def tile_attend_bsharedpower_k_kernel(
             return halves
 
         query_raw = load_halves(query, "query_raw")
+        pw_raw = sb.tile([P, PACK], F32, name="pw_raw")
+        nc.sync.dma_start(pw_raw[:], pw.rearrange("(p r) o -> p (r o)", r=PACK))
+        qs_sb = sb.tile([P, PACK], F32, name="qs_sb")
+        nc.sync.dma_start(qs_sb[:], qs.rearrange("(p r) o -> p (r o)", r=PACK))
+        nc.sync.dma_start(v_words[:].bitcast(I32), vals_words[0].bitcast(I32))
         for quad in range(4):
             nc.sync.dma_start(
                 v_plane[32 * quad : 32 * quad + 4, :].bitcast(I32),
                 vals_scales[0, 4 * quad : 4 * quad + 4, :].bitcast(I32),
             )
         gout_raw = load_halves(gout, "gout_raw")
-        pw_raw = sb.tile([P, PACK], F32, name="pw_raw")
-        nc.sync.dma_start(pw_raw[:], pw.rearrange("(p r) o -> p (r o)", r=PACK))
-        qs_sb = sb.tile([P, PACK], F32, name="qs_sb")
-        nc.sync.dma_start(qs_sb[:], qs.rearrange("(p r) o -> p (r o)", r=PACK))
         qrows_raw = sb.tile([P, PACK, D], F32, name="qrows_raw")
         nc.sync.dma_start(qrows_raw[:], qrows.rearrange("(p j) d -> p j d", j=PACK))
         places = sb.tile([P, I // 16], U16, name="places")
@@ -98,8 +101,8 @@ def tile_attend_bsharedpower_k_kernel(
 
         ident = sb.tile([P, P], F32, name="ident")
         make_identity(nc, ident[:])
-        windows = [sb.tile([P, U], F32, name=f"window{w}") for w in range(2)]
-        for w in range(2):
+        windows = [sb.tile([P, U], F32, name=f"window{w}") for w in range(3)]
+        for w in range(3):
             nc.gpsimd.memset(windows[w][:], 0.0)
 
         kg_words = sb.tile([P, I], U16, name="kg_words", align_bytes=64)
@@ -165,33 +168,33 @@ def tile_attend_bsharedpower_k_kernel(
         nc.scalar.activation(ls[:], s[:], ACT.Ln, bias=ln_floor[:])
 
         pw_zero = sb.tile([P, PACK], F32, name="pw_zero")
-        nc.vector.tensor_scalar(pw_zero[:], pw_raw[:], 0.0, PW_ZERO, ALU.is_equal, ALU.mult)
+        nc.gpsimd.tensor_scalar(pw_zero[:], pw_raw[:], 0.0, PW_ZERO, ALU.is_equal, ALU.mult)
         power = sb.tile([P, PACK], F32, name="power")
-        nc.vector.tensor_tensor(power[:], pw_raw[:], pw_zero[:], ALU.add)
+        nc.gpsimd.tensor_tensor(power[:], pw_raw[:], pw_zero[:], ALU.add)
         one_less = sb.tile([P, PACK], F32, name="one_less")
-        nc.vector.tensor_scalar(one_less[:], power[:], -1.0, 1.0, ALU.mult, ALU.add)
+        nc.gpsimd.tensor_scalar(one_less[:], power[:], -1.0, 1.0, ALU.mult, ALU.add)
         inv_power = sb.tile([P, PACK], F32, name="inv_power")
         nc.vector.reciprocal(inv_power[:], power[:])
         page_gain = sb.tile([P, PACK], F32, name="page_gain")
-        nc.vector.tensor_tensor(page_gain[:], one_less[:], inv_power[:], ALU.mult)
+        nc.gpsimd.tensor_tensor(page_gain[:], one_less[:], inv_power[:], ALU.mult)
         over_z = sb.tile([P, 2, PACK], F32, name="over_z")
-        nc.vector.tensor_tensor(over_z[:, 0, :], qs_sb[:], power[:], ALU.mult)
-        nc.vector.tensor_scalar(over_z[:, 1, :], inv_power[:], -1.0, None, ALU.mult)
+        nc.gpsimd.tensor_tensor(over_z[:, 0, :], qs_sb[:], power[:], ALU.mult)
+        nc.gpsimd.tensor_scalar(over_z[:, 1, :], inv_power[:], -1.0, 0.0, ALU.mult, ALU.add)
 
         gout_bf = sb.tile([P, PACK, P, PACK], BF16, name="gout_bf", align_bytes=64)
         for h in range(2):
             deal(nc.vector.tensor_copy, gout_raw[h], gout_bf, h)
 
         shift = sb.tile([P, PACK], F32, name="shift")
-        nc.vector.tensor_tensor(shift[:], neg_max[:], power[:], ALU.mult)
+        nc.gpsimd.tensor_tensor(shift[:], neg_max[:], power[:], ALU.mult)
         inv_z = sb.tile([P, PACK], F32, name="inv_z")
         nc.vector.reciprocal(inv_z[:], z[:])
         gains = sb.tile([P, 2, PACK], F32, name="gains")
-        nc.vector.tensor_tensor(gains[:], over_z[:], inv_z[:].unsqueeze(1).to_broadcast([P, 2, PACK]), ALU.mult)
+        nc.gpsimd.tensor_tensor(gains[:], over_z[:], inv_z[:].unsqueeze(1).to_broadcast([P, 2, PACK]), ALU.mult)
 
         page_term = sb.tile([P, PACK, G], F32, name="page_term")
         nc.vector.tensor_tensor(page_term[:], ls[:], over_pages(one_less[:]), ALU.mult)
-        expo = sb.tile([P, PACK, I], F32, name="expo", tag="expo", align_bytes=64)
+        expo = sb.tile([P, PACK, I], F32, name="expo")
         for r in range(PACK):
             nc.vector.scalar_tensor_tensor(
                 pages(expo[:, r, :]),
@@ -233,7 +236,7 @@ def tile_attend_bsharedpower_k_kernel(
                 accum_out=total[:, r : r + 1],
             )
         page_factor = sb.tile([P, PACK, G], F32, name="page_factor")
-        nc.vector.tensor_tensor(page_factor[:], inv_s[:], over_pages(page_gain[:]), ALU.mult)
+        nc.gpsimd.tensor_tensor(page_factor[:], inv_s[:], over_pages(page_gain[:]), ALU.mult)
         row_term = sb.tile([P, PACK], F32, name="row_term")
         nc.vector.tensor_tensor(row_term[:], total[:], gains[:, 1, :], ALU.mult)
         page_sum = sb.tile([P, PACK, G], F32, name="page_sum")
@@ -253,11 +256,16 @@ def tile_attend_bsharedpower_k_kernel(
                 ALU.mult,
             )
 
-        qrows_bf = sb.tile([P, D, PACK], BF16, name="qrows_bf", tag="expo", align_bytes=64)
-        nc.scalar.copy(
-            qrows_bf[:].rearrange("p (c i) j -> p c j i", i=4),
-            qrows_raw[:].rearrange("p j (c i) -> p c j i", i=4),
-        )
+        qrows_bf = sb.tile([P, D, PACK], BF16, name="qrows_bf", align_bytes=64)
+        for t in range(4):
+            nc.gpsimd.tensor_scalar(
+                qrows_bf[:, t * P : (t + 1) * P, :],
+                qrows_raw[:, :, t * P : (t + 1) * P].rearrange("p j d -> p d j"),
+                1.0,
+                0.0,
+                ALU.mult,
+                ALU.add,
+            )
         r_codes = sb.tile([P, D], U32, name="r_codes", align_bytes=64)
         r_plane = sb.tile([P, D], U8, name="r_plane", align_bytes=64)
 
@@ -287,9 +295,22 @@ def tile_attend_bsharedpower_k_kernel(
             out=gs_codes[:].bitcast(FP8X4), scales=gs_plane[:], in_=gs[:].rearrange("p i r -> p (i r)")
         )
 
+        fade_ps = bank(3, "fade_ps")
+        nc.tensor.transpose(fade_ps[:, 0:P], fade_rows[:], ident[:])
+        fade_cols = sb.tile([P, U // P], F32, name="fade_cols")
+        nc.scalar.copy(fade_cols[:], fade_ps[:, 0 : U // P])
+        faded_t = [sb.tile([P, D], F32, name=f"faded_t{c}") for c in range(U // P)]
+        for c in range(U // P):
+            turned = bank(TURN_BANKS[c % 4], f"turned{c}")
+            for t in range(4):
+                nc.tensor.transpose(
+                    turned[:, t * P : (t + 1) * P], old_sb[c // 4][:, t, (c % 4) * P : (c % 4 + 1) * P], ident[:]
+                )
+            nc.scalar.activation(faded_t[c][:], turned[:], ACT.Copy, scale=fade_cols[:, c : c + 1])
+
         gk = [sb.tile([P, I], F32, name=f"gk{t}") for t in range(4)]
         for t in range(4):
-            gk_ps = bank(t % 2, f"gk_ps{t}")
+            gk_ps = bank(TURN_BANKS[t], f"gk_ps{t}")
             nc.tensor.matmul_mx(
                 out=gk_ps[:, 0:I],
                 lhsT=r_codes[:, t * P : (t + 1) * P].bitcast(FP8X4),
@@ -301,24 +322,11 @@ def tile_attend_bsharedpower_k_kernel(
             )
             nc.scalar.copy(gk[t][:], gk_ps[:, 0:I])
 
-        fade_ps = bank(3, "fade_ps")
-        nc.tensor.transpose(fade_ps[:, 0:P], fade_rows[:], ident[:])
-        fade_cols = sb.tile([P, U // P], F32, name="fade_cols")
-        nc.scalar.copy(fade_cols[:], fade_ps[:, 0 : U // P])
-        faded_t = [sb.tile([P, D], F32, name=f"faded_t{c}") for c in range(U // P)]
-        for c in range(U // P):
-            turned = bank(7 - c % 2, f"turned{c}")
-            for t in range(4):
-                nc.tensor.transpose(
-                    turned[:, t * P : (t + 1) * P], old_sb[c // 4][:, t, (c % 4) * P : (c % 4 + 1) * P], ident[:]
-                )
-            nc.scalar.activation(faded_t[c][:], turned[:], ACT.Copy, scale=fade_cols[:, c : c + 1])
-
         def scatter(t):
-            nc.vector.tensor_copy(windows[t % 2][:].indirect(places[:]), gk[t][:])
+            nc.vector.tensor_copy(windows[min(t, 2)][:].indirect(places[:]), gk[t][:])
 
         def turn_back(t, h):
-            faded = bank(2 + (2 * t + h) % 6, f"faded{t}_{h}")
+            faded = bank(BACK_BANKS[2 * t + h], f"faded{t}_{h}")
             for c in range(4):
                 nc.tensor.transpose(
                     faded[:, c * P : (c + 1) * P], faded_t[4 * h + c][:, t * P : (t + 1) * P], ident[:]
@@ -330,11 +338,14 @@ def tile_attend_bsharedpower_k_kernel(
             for h in range(2):
                 cols = slice(h * BANK, (h + 1) * BANK)
                 faded = turn_back(t, h)
-                nc.vector.tensor_tensor(result[:, cols], faded[:], windows[t % 2][:, cols], ALU.add)
+                if 2 * t + h < ON_GPSIMD:
+                    faded_sb = sb.tile([P, BANK], F32, name=f"faded_sb{t}_{h}")
+                    nc.scalar.copy(faded_sb[:], faded[:])
+                    nc.gpsimd.tensor_tensor(result[:, cols], faded_sb[:], windows[t][:, cols], ALU.add)
+                else:
+                    nc.vector.tensor_tensor(result[:, cols], faded[:], windows[2][:, cols], ALU.add)
                 nc.sync.dma_start(out[t * P : (t + 1) * P, cols], result[:, cols])
 
-        scatter(0)
-        for t in range(1, 4):
+        for t in range(4):
             scatter(t)
-            finish(t - 1)
-        finish(3)
+            finish(t)

@@ -25,9 +25,9 @@ HALF = Q // 2
 BANK = 512
 LN_FLOOR = 2.0**-60
 PW_ZERO = 2.0**-60
-ON_GPSIMD = 4
 TURN_BANKS = (6, 7, 0, 1)
-BACK_BANKS = (2, 6, 7, 0, 1, 6, 7, 0)
+WINDOW_OF = (0, 1, 2, 1)
+ADD_ON_VECTOR = ((1, 1), (3, 0), (3, 1))
 
 
 def tile_attend_bsharedpower_k_kernel(
@@ -61,58 +61,56 @@ def tile_attend_bsharedpower_k_kernel(
 
         slots = sb.tile([P, I // 16], U16, name="slots")
         nc.sync.dma_start(slots[:], offs)
+        pw_raw = sb.tile([P, PACK], F32, name="pw_raw")
+        nc.scalar.dma_start(pw_raw[:], pw.rearrange("(p r) o -> p (r o)", r=PACK))
+        qs_sb = sb.tile([P, PACK], F32, name="qs_sb")
+        nc.scalar.dma_start(qs_sb[:], qs.rearrange("(p r) o -> p (r o)", r=PACK))
         k_words = sb.tile([P, T], U16, name="k_words", align_bytes=64)
         v_words = sb.tile([P, T], U16, name="v_words", align_bytes=64)
         nc.sync.dma_start(k_words[:].bitcast(I32), keys_words[0].bitcast(I32))
+
+        def load_half(src, name, h):
+            raw = sb.tile([P, PACK, HALF], F32, name=f"{name}{h}")
+            nc.sync.dma_start(raw[:], src.rearrange("(p j) q -> p j q", j=PACK)[:, :, h * HALF : (h + 1) * HALF])
+            return raw
+
+        query_raw = [load_half(query, "query_raw", 0)]
         for quad in range(4):
             nc.sync.dma_start(
                 k_plane[32 * quad : 32 * quad + 4, :].bitcast(I32),
                 keys_scales[0, 4 * quad : 4 * quad + 4, :].bitcast(I32),
             )
-
-        def load_halves(src, name):
-            rows = src.rearrange("(p j) q -> p j q", j=PACK)
-            halves = [sb.tile([P, PACK, HALF], F32, name=f"{name}{h}") for h in range(2)]
-            for h in range(2):
-                nc.sync.dma_start(halves[h][:], rows[:, :, h * HALF : (h + 1) * HALF])
-            return halves
-
-        query_raw = load_halves(query, "query_raw")
-        pw_raw = sb.tile([P, PACK], F32, name="pw_raw")
-        nc.sync.dma_start(pw_raw[:], pw.rearrange("(p r) o -> p (r o)", r=PACK))
-        qs_sb = sb.tile([P, PACK], F32, name="qs_sb")
-        nc.sync.dma_start(qs_sb[:], qs.rearrange("(p r) o -> p (r o)", r=PACK))
+        query_raw.append(load_half(query, "query_raw", 1))
         nc.sync.dma_start(v_words[:].bitcast(I32), vals_words[0].bitcast(I32))
+        gout_raw = [load_half(gout, "gout_raw", h) for h in range(2)]
         for quad in range(4):
             nc.sync.dma_start(
                 v_plane[32 * quad : 32 * quad + 4, :].bitcast(I32),
                 vals_scales[0, 4 * quad : 4 * quad + 4, :].bitcast(I32),
             )
-        gout_raw = load_halves(gout, "gout_raw")
         qrows_raw = sb.tile([P, PACK, D], F32, name="qrows_raw")
         nc.sync.dma_start(qrows_raw[:], qrows.rearrange("(p j) d -> p j d", j=PACK))
-        places = sb.tile([P, I // 16], U16, name="places")
-        nc.sync.dma_start(places[:], offs4)
         nc.sync.dma_start(fade_rows[0 : U // P, :], fade.rearrange("o (c u) -> (o c) u", u=P))
         old_rows = old.rearrange("(t p) u -> p t u", p=P)
         old_sb = [sb.tile([P, 4, BANK], F32, name=f"old_sb{h}") for h in range(2)]
         for h in range(2):
             nc.sync.dma_start(old_sb[h][:], old_rows[:, :, h * BANK : (h + 1) * BANK])
+        places = sb.tile([P, I // 16], U16, name="places")
+        nc.sync.dma_start(places[:], offs4)
 
         ident = sb.tile([P, P], F32, name="ident")
         make_identity(nc, ident[:])
         windows = [sb.tile([P, U], F32, name=f"window{w}") for w in range(3)]
-        for w in range(3):
-            nc.gpsimd.memset(windows[w][:], 0.0)
+        for w in range(2):
+            nc.vector.memset(windows[w][:].bitcast(I32), 0)
+        nc.gpsimd.memset(windows[2][:].bitcast(I32), 0)
 
         kg_words = sb.tile([P, I], U16, name="kg_words", align_bytes=64)
         vg_words = sb.tile([P, I], U16, name="vg_words", align_bytes=64)
         kg_plane = sb.tile([P, I], U8, name="kg_plane", align_bytes=64)
         vg_plane = sb.tile([P, I], U8, name="vg_plane", align_bytes=64)
         nc.vector.tensor_copy(kg_words[:], k_words[:].indirect(slots[:]))
-        nc.vector.tensor_copy(vg_words[:], v_words[:].indirect(slots[:]))
         nc.vector.tensor_copy(kg_plane[:], k_plane[:].indirect(slots[:]))
-        nc.vector.tensor_copy(vg_plane[:], v_plane[:].indirect(slots[:]))
 
         def deal(copy, raw, grouped, h):
             s0 = h * HALF // PACK
@@ -132,7 +130,7 @@ def tile_attend_bsharedpower_k_kernel(
                 )
             return codes, plane
 
-        query_bf = sb.tile([P, PACK, P, PACK], BF16, name="query_bf", align_bytes=64)
+        query_bf = sb.tile([P, PACK, P, PACK], BF16, name="query_bf", tag="grouped", align_bytes=64)
         deal(nc.scalar.copy, query_raw[0], query_bf, 0)
         deal(nc.vector.tensor_copy, query_raw[1], query_bf, 1)
         q_codes, q_plane = quantise(query_bf, "query")
@@ -181,9 +179,19 @@ def tile_attend_bsharedpower_k_kernel(
         nc.gpsimd.tensor_tensor(over_z[:, 0, :], qs_sb[:], power[:], ALU.mult)
         nc.gpsimd.tensor_scalar(over_z[:, 1, :], inv_power[:], -1.0, 0.0, ALU.mult, ALU.add)
 
-        gout_bf = sb.tile([P, PACK, P, PACK], BF16, name="gout_bf", align_bytes=64)
-        for h in range(2):
-            deal(nc.vector.tensor_copy, gout_raw[h], gout_bf, h)
+        nc.vector.tensor_copy(vg_words[:], v_words[:].indirect(slots[:]))
+        nc.vector.tensor_copy(vg_plane[:], v_plane[:].indirect(slots[:]))
+        gout_bf = sb.tile([P, PACK, P, PACK], BF16, name="gout_bf", tag="grouped", align_bytes=64)
+        for r in range(PACK):
+            nc.gpsimd.tensor_scalar(
+                gout_bf[:, r, 0 : HALF // PACK, :],
+                gout_raw[0][:].rearrange("p j (s r) -> p r s j", r=PACK)[:, r, :, :],
+                1.0,
+                0.0,
+                ALU.mult,
+                ALU.add,
+            )
+        deal(nc.vector.tensor_copy, gout_raw[1], gout_bf, 1)
 
         shift = sb.tile([P, PACK], F32, name="shift")
         nc.gpsimd.tensor_tensor(shift[:], neg_max[:], power[:], ALU.mult)
@@ -322,30 +330,21 @@ def tile_attend_bsharedpower_k_kernel(
             )
             nc.scalar.copy(gk[t][:], gk_ps[:, 0:I])
 
-        def scatter(t):
-            nc.vector.tensor_copy(windows[min(t, 2)][:].indirect(places[:]), gk[t][:])
-
-        def turn_back(t, h):
-            faded = bank(BACK_BANKS[2 * t + h], f"faded{t}_{h}")
-            for c in range(4):
-                nc.tensor.transpose(
-                    faded[:, c * P : (c + 1) * P], faded_t[4 * h + c][:, t * P : (t + 1) * P], ident[:]
-                )
-            return faded
-
-        def finish(t):
+        for t in range(4):
+            window = windows[WINDOW_OF[t]]
+            nc.vector.tensor_copy(window[:].indirect(places[:]), gk[t][:])
             result = sb.tile([P, U], F32, name=f"result{t}")
             for h in range(2):
                 cols = slice(h * BANK, (h + 1) * BANK)
-                faded = turn_back(t, h)
-                if 2 * t + h < ON_GPSIMD:
+                faded = bank(TURN_BANKS[(2 * t + h) % 4], f"faded{t}_{h}")
+                for c in range(4):
+                    nc.tensor.transpose(
+                        faded[:, c * P : (c + 1) * P], faded_t[4 * h + c][:, t * P : (t + 1) * P], ident[:]
+                    )
+                if (t, h) in ADD_ON_VECTOR:
+                    nc.vector.tensor_tensor(result[:, cols], faded[:], window[:, cols], ALU.add)
+                else:
                     faded_sb = sb.tile([P, BANK], F32, name=f"faded_sb{t}_{h}")
                     nc.scalar.copy(faded_sb[:], faded[:])
-                    nc.gpsimd.tensor_tensor(result[:, cols], faded_sb[:], windows[t][:, cols], ALU.add)
-                else:
-                    nc.vector.tensor_tensor(result[:, cols], faded[:], windows[2][:, cols], ALU.add)
+                    nc.gpsimd.tensor_tensor(result[:, cols], faded_sb[:], window[:, cols], ALU.add)
                 nc.sync.dma_start(out[t * P : (t + 1) * P, cols], result[:, cols])
-
-        for t in range(4):
-            scatter(t)
-            finish(t)

@@ -81,8 +81,9 @@ def tile_attend_bsharedpower_k_kernel(
                 keys_scales[0, 4 * quad : 4 * quad + 4, :].bitcast(I32),
             )
         query_raw.append(load_half(query, "query_raw", 1))
+        gout_raw = [load_half(gout, "gout_raw", 0)]
         nc.sync.dma_start(v_words[:].bitcast(I32), vals_words[0].bitcast(I32))
-        gout_raw = [load_half(gout, "gout_raw", h) for h in range(2)]
+        gout_raw.append(load_half(gout, "gout_raw", 1))
         for quad in range(4):
             nc.sync.dma_start(
                 v_plane[32 * quad : 32 * quad + 4, :].bitcast(I32),
@@ -112,28 +113,29 @@ def tile_attend_bsharedpower_k_kernel(
         nc.vector.tensor_copy(kg_words[:], k_words[:].indirect(slots[:]))
         nc.vector.tensor_copy(kg_plane[:], k_plane[:].indirect(slots[:]))
 
-        def deal(copy, raw, grouped, h):
-            s0 = h * HALF // PACK
+        def deal(copy, raw, grouped, h, first, count):
+            s0 = h * HALF // PACK + first
             copy(
-                grouped[:, :, s0 : s0 + HALF // PACK, :].rearrange("p r s j -> p s j r"),
-                raw[:].rearrange("p j (s r) -> p s j r", r=PACK),
+                grouped[:, :, s0 : s0 + count, :].rearrange("p r s j -> p s j r"),
+                raw[:].rearrange("p j (s r) -> p s j r", r=PACK)[:, first : first + count, :, :],
             )
 
-        def quantise(grouped, name):
+        def quantise(grouped, name, step):
             codes = sb.tile([P, PACK, P], U32, name=f"{name}_codes", align_bytes=64)
             plane = sb.tile([P, PACK, P], U8, name=f"{name}_plane", align_bytes=64)
-            for r in range(PACK):
+            for r in range(0, PACK, step):
                 nc.vector.quantize_mx(
-                    out=codes[:, r, :].bitcast(FP8X4),
-                    scales=plane[:, r, :],
-                    in_=grouped[:, r, :, :].rearrange("p s j -> p (s j)"),
+                    out=codes[:, r : r + step, :].rearrange("p r s -> p (r s)").bitcast(FP8X4),
+                    scales=plane[:, r : r + step, :].rearrange("p r s -> p (r s)"),
+                    in_=grouped[:, r : r + step, :, :].rearrange("p r s j -> p (r s j)"),
                 )
             return codes, plane
 
         query_bf = sb.tile([P, PACK, P, PACK], BF16, name="query_bf", tag="grouped", align_bytes=64)
-        deal(nc.scalar.copy, query_raw[0], query_bf, 0)
-        deal(nc.vector.tensor_copy, query_raw[1], query_bf, 1)
-        q_codes, q_plane = quantise(query_bf, "query")
+        deal(nc.scalar.copy, query_raw[0], query_bf, 0, 0, 64)
+        deal(nc.vector.tensor_copy, query_raw[1], query_bf, 1, 0, 36)
+        deal(nc.scalar.copy, query_raw[1], query_bf, 1, 36, 28)
+        q_codes, q_plane = quantise(query_bf, "query", 1)
         a_ps = [bank(r, f"a_ps{r}") for r in range(PACK)]
         for r in range(PACK):
             nc.tensor.matmul_mx(
@@ -191,7 +193,7 @@ def tile_attend_bsharedpower_k_kernel(
                 ALU.mult,
                 ALU.add,
             )
-        deal(nc.vector.tensor_copy, gout_raw[1], gout_bf, 1)
+        deal(nc.vector.tensor_copy, gout_raw[1], gout_bf, 1, 0, 64)
 
         shift = sb.tile([P, PACK], F32, name="shift")
         nc.gpsimd.tensor_tensor(shift[:], neg_max[:], power[:], ALU.mult)
@@ -212,7 +214,7 @@ def tile_attend_bsharedpower_k_kernel(
                 ALU.mult,
                 ALU.add,
             )
-        g_codes, g_plane = quantise(gout_bf, "gout")
+        g_codes, g_plane = quantise(gout_bf, "gout", PACK)
         c_ps = [bank(4 + h, f"c_ps{h}") for h in range(2)]
         for r in range(PACK):
             nc.tensor.matmul_mx(
@@ -244,7 +246,8 @@ def tile_attend_bsharedpower_k_kernel(
                 accum_out=total[:, r : r + 1],
             )
         page_factor = sb.tile([P, PACK, G], F32, name="page_factor")
-        nc.gpsimd.tensor_tensor(page_factor[:], inv_s[:], over_pages(page_gain[:]), ALU.mult)
+        for r in range(PACK):
+            nc.scalar.activation(page_factor[:, r, :], inv_s[:, r, :], ACT.Copy, scale=page_gain[:, r : r + 1])
         row_term = sb.tile([P, PACK], F32, name="row_term")
         nc.vector.tensor_tensor(row_term[:], total[:], gains[:, 1, :], ALU.mult)
         page_sum = sb.tile([P, PACK, G], F32, name="page_sum")
@@ -264,7 +267,7 @@ def tile_attend_bsharedpower_k_kernel(
                 ALU.mult,
             )
 
-        qrows_bf = sb.tile([P, D, PACK], BF16, name="qrows_bf", align_bytes=64)
+        qrows_bf = sb.tile([P, D, PACK], BF16, name="qrows_bf", tag="grouped", align_bytes=64)
         for t in range(4):
             nc.gpsimd.tensor_scalar(
                 qrows_bf[:, t * P : (t + 1) * P, :],
@@ -274,10 +277,8 @@ def tile_attend_bsharedpower_k_kernel(
                 ALU.mult,
                 ALU.add,
             )
-        r_codes = sb.tile([P, D], U32, name="r_codes", align_bytes=64)
-        r_plane = sb.tile([P, D], U8, name="r_plane", align_bytes=64)
 
-        through = sb.tile([P, PACK, I], F32, name="through")
+        through = sb.tile([P, PACK, I], F32, name="through", tag="through", align_bytes=64)
         for r in range(PACK):
             nc.vector.scalar_tensor_tensor(
                 pages(through[:, r, :]),
@@ -294,14 +295,21 @@ def tile_attend_bsharedpower_k_kernel(
             through[:].rearrange("p r (c i) -> p c r i", i=4),
             ALU.add,
         )
-        nc.vector.quantize_mx(
-            out=r_codes[:].bitcast(FP8X4), scales=r_plane[:], in_=qrows_bf[:].rearrange("p d j -> p (d j)")
-        )
+
+        def quantise_rows(h, tag):
+            codes = sb.tile([P, D // 2], U32, name=f"r_codes{h}", tag=tag, align_bytes=64)
+            plane = sb.tile([P, D // 2], U8, name=f"r_plane{h}", align_bytes=64)
+            rows = qrows_bf[:, h * D // 2 : (h + 1) * D // 2, :]
+            nc.vector.quantize_mx(out=codes[:].bitcast(FP8X4), scales=plane[:], in_=rows.rearrange("p d j -> p (d j)"))
+            return codes, plane
+
+        r_mx = [quantise_rows(0, "r_codes0")]
         gs_codes = sb.tile([P, I], U32, name="gs_codes", align_bytes=64)
         gs_plane = sb.tile([P, I], U8, name="gs_plane", align_bytes=64)
         nc.vector.quantize_mx(
             out=gs_codes[:].bitcast(FP8X4), scales=gs_plane[:], in_=gs[:].rearrange("p i r -> p (i r)")
         )
+        r_mx.append(quantise_rows(1, "through"))
 
         fade_ps = bank(3, "fade_ps")
         nc.tensor.transpose(fade_ps[:, 0:P], fade_rows[:], ident[:])
@@ -321,8 +329,8 @@ def tile_attend_bsharedpower_k_kernel(
             gk_ps = bank(TURN_BANKS[t], f"gk_ps{t}")
             nc.tensor.matmul_mx(
                 out=gk_ps[:, 0:I],
-                lhsT=r_codes[:, t * P : (t + 1) * P].bitcast(FP8X4),
-                lhsT_scale=r_plane[:, t * P : (t + 1) * P],
+                lhsT=r_mx[t // 2][0][:, t % 2 * P : (t % 2 + 1) * P].bitcast(FP8X4),
+                lhsT_scale=r_mx[t // 2][1][:, t % 2 * P : (t % 2 + 1) * P],
                 rhs=gs_codes[:].bitcast(FP8X4),
                 rhs_scale=gs_plane[:],
                 start=True,

@@ -184,15 +184,16 @@ def tile_attend_bsharedpower_k_kernel(
         nc.vector.tensor_copy(vg_words[:], v_words[:].indirect(slots[:]))
         nc.vector.tensor_copy(vg_plane[:], v_plane[:].indirect(slots[:]))
         gout_bf = sb.tile([P, PACK, P, PACK], BF16, name="gout_bf", tag="grouped", align_bytes=64)
-        for r in range(PACK):
+        for r in range(0, PACK, 2):
             nc.gpsimd.tensor_scalar(
-                gout_bf[:, r, 0 : HALF // PACK, :],
-                gout_raw[0][:].rearrange("p j (s r) -> p r s j", r=PACK)[:, r, :, :],
+                gout_bf[:, r : r + 2, 0:32, :],
+                gout_raw[0][:].rearrange("p j (s r) -> p r s j", r=PACK)[:, r : r + 2, 0:32, :],
                 1.0,
                 0.0,
                 ALU.mult,
                 ALU.add,
             )
+        deal(nc.vector.tensor_copy, gout_raw[0], gout_bf, 0, 32, 32)
         deal(nc.vector.tensor_copy, gout_raw[1], gout_bf, 1, 0, 64)
 
         shift = sb.tile([P, PACK], F32, name="shift")

from contextlib import ExitStack

import concourse.mybir as mybir
from concourse.masks import make_identity

D, E, T, I, Q, G, U = 512, 512, 1024, 256, 512, 32, 1024
FLOPS = 2 * Q * I * D + 2 * Q * I * E + 2 * D * I * Q

F32 = mybir.dt.float32
BF16 = mybir.dt.bfloat16
I32 = mybir.dt.int32
U32 = mybir.dt.uint32
U16 = mybir.dt.uint16
U8 = mybir.dt.uint8
FP8X4 = mybir.dt.float8_e4m3fn_x4
FP4X4 = mybir.dt.float4_e2m1fn_x4
ALU = mybir.AluOpType
ACT = mybir.ActivationFunctionType
AX = mybir.AxisListType

P = 128
PACK = 4
PAGE = I // G
HALF = Q // 2
BANK = 512
LN_FLOOR = 2.0**-60
PW_ZERO = 2.0**-60
TURN_BANKS = (6, 7, 0, 1)
WINDOW_OF = (0, 1, 2, 1)
ADD_ON_VECTOR = ((1, 1), (3, 0), (3, 1))


def tile_attend_bsharedpower_k_kernel(
    tc, query, keys_words, keys_scales, pw, gout, vals_words, vals_scales, qs, qrows, old, fade, offs, offs4, out
):
    nc = tc.nc
    with ExitStack() as ctx:
        sb = ctx.enter_context(tc.tile_pool(name="sb", bufs=1))
        ps = ctx.enter_context(tc.psum_pool(name="ps", bufs=1))

        def bank(k, name):
            return ps.tile([P, BANK], F32, name=name, tag=f"bank{k}")

        def pages(ap):
            return ap.rearrange("p (g j) -> p g j", j=PAGE)

        def over_slots(ap):
            return ap.unsqueeze(2).to_broadcast([P, G, PAGE])

        def over_pages(ap):
            return ap.unsqueeze(2).to_broadcast([P, ap.shape[1], G])

        k_plane = sb.tile([P, T], U8, name="k_plane", align_bytes=64)
        v_plane = sb.tile([P, T], U8, name="v_plane", align_bytes=64)
        nc.gpsimd.memset(k_plane[:].bitcast(I32), 0)
        nc.gpsimd.memset(v_plane[:].bitcast(I32), 0)
        fade_rows = sb.tile([P, P], F32, name="fade_rows")
        nc.vector.memset(fade_rows[:], 0.0)
        ln_floor = sb.tile([P, 1], F32, name="ln_floor")
        nc.vector.memset(ln_floor[:], LN_FLOOR)

        slots = sb.tile([P, I // 16], U16, name="slots")
        nc.sync.dma_start(slots[:], offs)
        pw_raw = sb.tile([P, PACK], F32, name="pw_raw")
        nc.scalar.dma_start(pw_raw[:], pw.rearrange("(p r) o -> p (r o)", r=PACK))
        qs_sb = sb.tile([P, PACK], F32, name="qs_sb")
        nc.scalar.dma_start(qs_sb[:], qs.rearrange("(p r) o -> p (r o)", r=PACK))
        k_words = sb.tile([P, T], U16, name="k_words", align_bytes=64)
        v_words = sb.tile([P, T], U16, name="v_words", align_bytes=64)
        nc.sync.dma_start(k_words[:].bitcast(I32), keys_words[0].bitcast(I32))

        def load_half(src, name, h):
            raw = sb.tile([P, PACK, HALF], F32, name=f"{name}{h}")
            nc.sync.dma_start(raw[:], src.rearrange("(p j) q -> p j q", j=PACK)[:, :, h * HALF : (h + 1) * HALF])
            return raw

        query_raw = [load_half(query, "query_raw", 0)]
        for quad in range(4):
            nc.sync.dma_start(
                k_plane[32 * quad : 32 * quad + 4, :].bitcast(I32),
                keys_scales[0, 4 * quad : 4 * quad + 4, :].bitcast(I32),
            )
        query_raw.append(load_half(query, "query_raw", 1))
        gout_raw = [load_half(gout, "gout_raw", 0)]
        nc.sync.dma_start(v_words[:].bitcast(I32), vals_words[0].bitcast(I32))
        gout_raw.append(load_half(gout, "gout_raw", 1))
        for quad in range(4):
            nc.sync.dma_start(
                v_plane[32 * quad : 32 * quad + 4, :].bitcast(I32),
                vals_scales[0, 4 * quad : 4 * quad + 4, :].bitcast(I32),
            )
        qrows_raw = sb.tile([P, PACK, D], F32, name="qrows_raw")
        nc.sync.dma_start(qrows_raw[:], qrows.rearrange("(p j) d -> p j d", j=PACK))
        nc.sync.dma_start(fade_rows[0 : U // P, :], fade.rearrange("o (c u) -> (o c) u", u=P))
        old_rows = old.rearrange("(t p) u -> p t u", p=P)
        old_sb = [sb.tile([P, 4, BANK], F32, name=f"old_sb{h}") for h in range(2)]
        for h in range(2):
            nc.sync.dma_start(old_sb[h][:], old_rows[:, :, h * BANK : (h + 1) * BANK])
        places = sb.tile([P, I // 16], U16, name="places")
        nc.sync.dma_start(places[:], offs4)

        ident = sb.tile([P, P], F32, name="ident")
        make_identity(nc, ident[:])
        windows = [sb.tile([P, U], F32, name=f"window{w}") for w in range(3)]
        for w in range(2):
            nc.vector.memset(windows[w][:].bitcast(I32), 0)
        nc.gpsimd.memset(windows[2][:].bitcast(I32), 0)

        kg_words = sb.tile([P, I], U16, name="kg_words", align_bytes=64)
        vg_words = sb.tile([P, I], U16, name="vg_words", align_bytes=64)
        kg_plane = sb.tile([P, I], U8, name="kg_plane", align_bytes=64)
        vg_plane = sb.tile([P, I], U8, name="vg_plane", align_bytes=64)
        nc.vector.tensor_copy(kg_words[:], k_words[:].indirect(slots[:]))
        nc.vector.tensor_copy(kg_plane[:], k_plane[:].indirect(slots[:]))

        def deal(copy, raw, grouped, h, first, count):
            s0 = h * HALF // PACK + first
            copy(
                grouped[:, :, s0 : s0 + count, :].rearrange("p r s j -> p s j r"),
                raw[:].rearrange("p j (s r) -> p s j r", r=PACK)[:, first : first + count, :, :],
            )

        def quantise(grouped, name, step):
            codes = sb.tile([P, PACK, P], U32, name=f"{name}_codes", align_bytes=64)
            plane = sb.tile([P, PACK, P], U8, name=f"{name}_plane", align_bytes=64)
            for r in range(0, PACK, step):
                nc.vector.quantize_mx(
                    out=codes[:, r : r + step, :].rearrange("p r s -> p (r s)").bitcast(FP8X4),
                    scales=plane[:, r : r + step, :].rearrange("p r s -> p (r s)"),
                    in_=grouped[:, r : r + step, :, :].rearrange("p r s j -> p (r s j)"),
                )
            return codes, plane

        query_bf = sb.tile([P, PACK, P, PACK], BF16, name="query_bf", tag="grouped", align_bytes=64)
        deal(nc.scalar.copy, query_raw[0], query_bf, 0, 0, 64)
        deal(nc.vector.tensor_copy, query_raw[1], query_bf, 1, 0, 36)
        deal(nc.scalar.copy, query_raw[1], query_bf, 1, 36, 28)
        q_codes, q_plane = quantise(query_bf, "query", 1)
        a_ps = [bank(r, f"a_ps{r}") for r in range(PACK)]
        for r in range(PACK):
            nc.tensor.matmul_mx(
                out=a_ps[r][:, 0:I],
                lhsT=q_codes[:, r, :].bitcast(FP8X4),
                lhsT_scale=q_plane[:, r, :],
                rhs=kg_words[:].bitcast(FP4X4),
                rhs_scale=kg_plane[:],
                start=True,
                stop=True,
            )

        neg_max = sb.tile([P, PACK], F32, name="neg_max")
        z = sb.tile([P, PACK], F32, name="z")
        x1 = sb.tile([P, PACK, I], F32, name="x1")
        for r in range(PACK):
            nc.vector.tensor_reduce(neg_max[:, r : r + 1], a_ps[r][:, 0:I], AX.X, ALU.max, negate=True)
            nc.scalar.activation(
                x1[:, r, :], a_ps[r][:, 0:I], ACT.Exp, bias=neg_max[:, r : r + 1], accum_out=z[:, r : r + 1]
            )
        s = sb.tile([P, PACK, G], F32, name="s")
        for h in range(2):
            nc.vector.tensor_reduce(
                s[:, 2 * h : 2 * h + 2, :].rearrange("p r g -> p (r g)"),
                x1[:, 2 * h : 2 * h + 2, :].rearrange("p r (g j) -> p (r g) j", j=PAGE),
                AX.X,
                ALU.add,
            )
        ls = sb.tile([P, PACK, G], F32, name="ls")
        nc.scalar.activation(ls[:], s[:], ACT.Ln, bias=ln_floor[:])

        pw_zero = sb.tile([P, PACK], F32, name="pw_zero")
        nc.gpsimd.tensor_scalar(pw_zero[:], pw_raw[:], 0.0, PW_ZERO, ALU.is_equal, ALU.mult)
        power = sb.tile([P, PACK], F32, name="power")
        nc.gpsimd.tensor_tensor(power[:], pw_raw[:], pw_zero[:], ALU.add)
        one_less = sb.tile([P, PACK], F32, name="one_less")
        nc.gpsimd.tensor_scalar(one_less[:], power[:], -1.0, 1.0, ALU.mult, ALU.add)
        inv_power = sb.tile([P, PACK], F32, name="inv_power")
        nc.vector.reciprocal(inv_power[:], power[:])
        page_gain = sb.tile([P, PACK], F32, name="page_gain")
        nc.gpsimd.tensor_tensor(page_gain[:], one_less[:], inv_power[:], ALU.mult)
        over_z = sb.tile([P, 2, PACK], F32, name="over_z")
        nc.gpsimd.tensor_tensor(over_z[:, 0, :], qs_sb[:], power[:], ALU.mult)
        nc.gpsimd.tensor_scalar(over_z[:, 1, :], inv_power[:], -1.0, 0.0, ALU.mult, ALU.add)

        nc.vector.tensor_copy(vg_words[:], v_words[:].indirect(slots[:]))
        nc.vector.tensor_copy(vg_plane[:], v_plane[:].indirect(slots[:]))
        gout_bf = sb.tile([P, PACK, P, PACK], BF16, name="gout_bf", tag="grouped", align_bytes=64)
        for r in range(0, PACK, 2):
            nc.gpsimd.tensor_scalar(
                gout_bf[:, r : r + 2, 0:32, :],
                gout_raw[0][:].rearrange("p j (s r) -> p r s j", r=PACK)[:, r : r + 2, 0:32, :],
                1.0,
                0.0,
                ALU.mult,
                ALU.add,
            )
        deal(nc.vector.tensor_copy, gout_raw[0], gout_bf, 0, 32, 32)
        deal(nc.vector.tensor_copy, gout_raw[1], gout_bf, 1, 0, 64)

        shift = sb.tile([P, PACK], F32, name="shift")
        nc.gpsimd.tensor_tensor(shift[:], neg_max[:], power[:], ALU.mult)
        inv_z = sb.tile([P, PACK], F32, name="inv_z")
        nc.vector.reciprocal(inv_z[:], z[:])
        gains = sb.tile([P, 2, PACK], F32, name="gains")
        nc.gpsimd.tensor_tensor(gains[:], over_z[:], inv_z[:].unsqueeze(1).to_broadcast([P, 2, PACK]), ALU.mult)

        page_term = sb.tile([P, PACK, G], F32, name="page_term")
        nc.vector.tensor_tensor(page_term[:], ls[:], over_pages(one_less[:]), ALU.mult)
        expo = sb.tile([P, PACK, I], F32, name="expo")
        for r in range(PACK):
            nc.vector.scalar_tensor_tensor(
                pages(expo[:, r, :]),
                pages(a_ps[r][:, 0:I]),
                power[:, r : r + 1],
                over_slots(page_term[:, r, :]),
                ALU.mult,
                ALU.add,
            )
        g_codes, g_plane = quantise(gout_bf, "gout", PACK)
        c_ps = [bank(4 + h, f"c_ps{h}") for h in range(2)]
        for r in range(PACK):
            nc.tensor.matmul_mx(
                out=c_ps[r // 2][:, (r % 2) * I : (r % 2 + 1) * I],
                lhsT=g_codes[:, r, :].bitcast(FP8X4),
                lhsT_scale=g_plane[:, r, :],
                rhs=vg_words[:].bitcast(FP4X4),
                rhs_scale=vg_plane[:],
                start=True,
                stop=True,
            )

        weight = sb.tile([P, PACK, I], F32, name="weight")
        for r in range(PACK):
            nc.scalar.activation(weight[:, r, :], expo[:, r, :], ACT.Exp, bias=shift[:, r : r + 1])
        inv_s = sb.tile([P, PACK, G], F32, name="inv_s")
        nc.scalar.activation(inv_s[:], ls[:], ACT.Exp, scale=-1.0)

        direct = sb.tile([P, PACK, I], F32, name="direct")
        total = sb.tile([P, PACK], F32, name="total")
        for r in range(PACK):
            nc.vector.scalar_tensor_tensor(
                direct[:, r, :],
                c_ps[r // 2][:, (r % 2) * I : (r % 2 + 1) * I],
                gains[:, 0, r : r + 1],
                weight[:, r, :],
                ALU.mult,
                ALU.mult,
                accum_out=total[:, r : r + 1],
            )
        page_factor = sb.tile([P, PACK, G], F32, name="page_factor")
        for r in range(PACK):
            nc.scalar.activation(page_factor[:, r, :], inv_s[:, r, :], ACT.Copy, scale=page_gain[:, r : r + 1])
        row_term = sb.tile([P, PACK], F32, name="row_term")
        nc.vector.tensor_tensor(row_term[:], total[:], gains[:, 1, :], ALU.mult)
        page_sum = sb.tile([P, PACK, G], F32, name="page_sum")
        page_grad = sb.tile([P, PACK, G], F32, name="page_grad")
        for h in range(2):
            nc.vector.tensor_reduce(
                page_sum[:, 2 * h : 2 * h + 2, :].rearrange("p r g -> p (r g)"),
                direct[:, 2 * h : 2 * h + 2, :].rearrange("p r (g j) -> p (r g) j", j=PAGE),
                AX.X,
                ALU.add,
            )
        for h in range(2):
            nc.vector.tensor_tensor(
                page_grad[:, 2 * h : 2 * h + 2, :],
                page_sum[:, 2 * h : 2 * h + 2, :],
                page_factor[:, 2 * h : 2 * h + 2, :],
                ALU.mult,
            )

        qrows_bf = sb.tile([P, D, PACK], BF16, name="qrows_bf", tag="grouped", align_bytes=64)
        for t in range(4):
            nc.gpsimd.tensor_scalar(
                qrows_bf[:, t * P : (t + 1) * P, :],
                qrows_raw[:, :, t * P : (t + 1) * P].rearrange("p j d -> p d j"),
                1.0,
                0.0,
                ALU.mult,
                ALU.add,
            )

        through = sb.tile([P, PACK, I], F32, name="through", tag="through", align_bytes=64)
        for r in range(PACK):
            nc.vector.scalar_tensor_tensor(
                pages(through[:, r, :]),
                over_slots(page_grad[:, r, :]),
                row_term[:, r : r + 1],
                pages(x1[:, r, :]),
                ALU.add,
                ALU.mult,
            )
        gs = sb.tile([P, I, PACK], BF16, name="gs", align_bytes=64)
        nc.vector.tensor_tensor(
            gs[:].rearrange("p (c i) r -> p c r i", i=4),
            direct[:].rearrange("p r (c i) -> p c r i", i=4),
            through[:].rearrange("p r (c i) -> p c r i", i=4),
            ALU.add,
        )

        def quantise_rows(h, tag):
            codes = sb.tile([P, D // 2], U32, name=f"r_codes{h}", tag=tag, align_bytes=64)
            plane = sb.tile([P, D // 2], U8, name=f"r_plane{h}", align_bytes=64)
            rows = qrows_bf[:, h * D // 2 : (h + 1) * D // 2, :]
            nc.vector.quantize_mx(out=codes[:].bitcast(FP8X4), scales=plane[:], in_=rows.rearrange("p d j -> p (d j)"))
            return codes, plane

        r_mx = [quantise_rows(0, "r_codes0")]
        gs_codes = sb.tile([P, I], U32, name="gs_codes", align_bytes=64)
        gs_plane = sb.tile([P, I], U8, name="gs_plane", align_bytes=64)
        nc.vector.quantize_mx(
            out=gs_codes[:].bitcast(FP8X4), scales=gs_plane[:], in_=gs[:].rearrange("p i r -> p (i r)")
        )
        r_mx.append(quantise_rows(1, "through"))

        fade_ps = bank(3, "fade_ps")
        nc.tensor.transpose(fade_ps[:, 0:P], fade_rows[:], ident[:])
        fade_cols = sb.tile([P, U // P], F32, name="fade_cols")
        nc.scalar.copy(fade_cols[:], fade_ps[:, 0 : U // P])
        faded_t = [sb.tile([P, D], F32, name=f"faded_t{c}") for c in range(U // P)]
        for c in range(U // P):
            turned = bank(TURN_BANKS[c % 4], f"turned{c}")
            for t in range(4):
                nc.tensor.transpose(
                    turned[:, t * P : (t + 1) * P], old_sb[c // 4][:, t, (c % 4) * P : (c % 4 + 1) * P], ident[:]
                )
            nc.scalar.activation(faded_t[c][:], turned[:], ACT.Copy, scale=fade_cols[:, c : c + 1])

        gk = [sb.tile([P, I], F32, name=f"gk{t}") for t in range(4)]
        for t in range(4):
            gk_ps = bank(TURN_BANKS[t], f"gk_ps{t}")
            nc.tensor.matmul_mx(
                out=gk_ps[:, 0:I],
                lhsT=r_mx[t // 2][0][:, t % 2 * P : (t % 2 + 1) * P].bitcast(FP8X4),
                lhsT_scale=r_mx[t // 2][1][:, t % 2 * P : (t % 2 + 1) * P],
                rhs=gs_codes[:].bitcast(FP8X4),
                rhs_scale=gs_plane[:],
                start=True,
                stop=True,
            )
            nc.scalar.copy(gk[t][:], gk_ps[:, 0:I])

        for t in range(4):
            window = windows[WINDOW_OF[t]]
            nc.vector.tensor_copy(window[:].indirect(places[:]), gk[t][:])
            result = sb.tile([P, U], F32, name=f"result{t}")
            for h in range(2):
                cols = slice(h * BANK, (h + 1) * BANK)
                faded = bank(TURN_BANKS[(2 * t + h) % 4], f"faded{t}_{h}")
                for c in range(4):
                    nc.tensor.transpose(
                        faded[:, c * P : (c + 1) * P], faded_t[4 * h + c][:, t * P : (t + 1) * P], ident[:]
                    )
                if (t, h) in ADD_ON_VECTOR:
                    nc.vector.tensor_tensor(result[:, cols], faded[:], window[:, cols], ALU.add)
                else:
                    faded_sb = sb.tile([P, BANK], F32, name=f"faded_sb{t}_{h}")
                    nc.scalar.copy(faded_sb[:], faded[:])
                    nc.gpsimd.tensor_tensor(result[:, cols], faded_sb[:], window[:, cols], ALU.add)
                nc.sync.dma_start(out[t * P : (t + 1) * P, cols], result[:, cols])
